import numpy as np
import ml_dtypes


def mxq(x, axis, fmt="e4m3"):
    dtype, down = {"e4m3": (ml_dtypes.float8_e4m3fn, 7), "e5m2": (ml_dtypes.float8_e5m2, 14)}[fmt]
    v = np.moveaxis(np.asarray(x, np.float32).astype(ml_dtypes.bfloat16).astype(np.float64), axis, -1)
    blocks = v.reshape(v.shape[:-1] + (-1, 32))
    amax = np.abs(blocks).max(-1, keepdims=True)
    byte = np.maximum(np.where(amax > 0, np.frexp(amax)[1] - 1 + 127, 0) - down, 1)
    scale = np.exp2(byte - 127.0)
    codes = (blocks / scale).astype(np.float32).astype(dtype).astype(np.float64)
    return np.moveaxis((codes * scale).reshape(v.shape), -1, axis)


WIDE = False


def mx_kscale(k):
    if not WIDE:
        return np.ones(k)
    levels = np.array([10, -10, 5, -5, 0])
    if k % 512:
        return np.exp2(np.random.permutation(np.resize(levels, k // 32))).repeat(32)
    a = np.empty((k // 512, 16))
    for p in range(k // 512):
        a[p, :8] = np.random.permutation(np.resize(levels, 8))
        for g in range(8):
            far = levels[np.abs(levels - a[p, g]) >= 10]
            a[p, g + 8] = far[np.random.randint(len(far))]
    return np.exp2(a.ravel()).repeat(32)


def f64(x):
    return np.asarray(x).astype(np.float64)


def striped(idx):
    return np.tile(np.asarray(idx).reshape(-1, 16).T, (8, 1)).astype(np.uint16)


def unstriped(offs):
    return offs[:16].T.reshape(-1).astype(np.int64)


E2M1 = np.array([0.0, 0.5, 1.0, 1.5, 2.0, 3.0, 4.0, 6.0, -0.0, -0.5, -1.0, -1.5, -2.0, -3.0, -4.0, -6.0])


def pack_weight(w, fmt):
    k, n = w.shape
    w = f64(np.asarray(w, np.float32).astype(ml_dtypes.bfloat16)).reshape(k // 32, 32, n)
    amax = np.abs(w).max(1)
    if fmt == "e4m3":
        byte = np.frexp(amax)[1] - 1 + 127 - 7
    else:
        mant, ex = np.frexp(amax / 6.0)
        byte = np.where(mant > 0.5, ex, ex - 1) + 127
    byte = np.clip(np.where(amax > 0, byte, 1), 1, 254)
    scaled = (w * np.exp2(127.0 - byte)[:, None, :]).reshape(k, n).astype(np.float32)
    by_word = np.ascontiguousarray(scaled.reshape(k // 512, 128, 4, n).transpose(0, 1, 3, 2))
    if fmt == "e4m3":
        words = by_word.astype(ml_dtypes.float8_e4m3fn).view(np.uint8)
    else:
        c = by_word.astype(ml_dtypes.float4_e2m1fn).view(np.uint8) & 0xF
        words = (c[..., 0::2] | (c[..., 1::2] << 4)).reshape(k // 512, 128, 2 * n)
    return np.ascontiguousarray(words), np.ascontiguousarray(byte.astype(np.uint8).reshape(k // 512, 16, n))


def unpack_weight(words, scales, fmt):
    g, _, n = scales.shape
    words = np.ascontiguousarray(words).reshape(g, 128, n, -1)
    if fmt == "e4m3":
        vals = words.view(ml_dtypes.float8_e4m3fn).astype(np.float64)
    else:
        nib = np.empty((g, 128, n, 4), np.uint8)
        nib[..., 0::2] = words & 0xF
        nib[..., 1::2] = words >> 4
        vals = E2M1[nib]
    vals = vals * np.repeat(np.exp2(scales.astype(np.float64) - 127.0), 8, axis=1)[..., None]
    return vals.transpose(0, 1, 3, 2).reshape(g * 512, n)


D, E, T, I, Q = 512, 512, 2048, 512, 128


def setup_inputs():
    n = np.random.standard_normal
    idx = np.random.permutation(T)[:I]
    fd = mx_kscale(D)
    fe = mx_kscale(E)
    keysp = pack_weight(n((D, T)) / fd[:, None], "e2m1")
    valsp = pack_weight(n((E, T)) / fe[:, None], "e2m1")
    return {
        "query": (n((D, Q)) * 0.7 / np.sqrt(D) * fd[:, None]).astype(np.float32),
        "query2": (n((D, Q)) * 0.7 / np.sqrt(D) * fd[:, None]).astype(np.float32),
        "keys_words": keysp[0],
        "keys_scales": keysp[1],
        "sharp": (np.random.uniform(0.3, 1.2, (Q, 1))).astype(np.float32),
        "gout": (n((E, Q)) * 1 / np.sqrt(E) * fe[:, None]).astype(np.float32),
        "vals_words": valsp[0],
        "vals_scales": valsp[1],
        "old": (0.5 * n((Q, T))).astype(np.float32),
        "offs": striped(idx),
    }


def reference(query, query2, keys_words, keys_scales, sharp, gout, vals_words, vals_scales, old, offs):
    idx = unstriped(offs)
    keysu = unpack_weight(keys_words, keys_scales, "e2m1")
    valsu = unpack_weight(vals_words, vals_scales, "e2m1")
    queryq = mxq(f64(query), 0, "e4m3")
    keysidxg = keysu[:, idx]
    a = queryq.T @ keysidxg
    query2q = mxq(f64(query2), 0, "e4m3")
    b = query2q.T @ keysidxg
    dl = a - b
    p = np.exp(a * 0.5) / (np.square(dl) * f64(sharp) + 1.0)
    z = np.sum(p, axis=1, keepdims=True)
    goutq = mxq(f64(gout), 0, "e4m3")
    valsidxg = valsu[:, idx]
    c0 = goutq.T @ valsidxg
    dz = np.sum(c0 * p / np.square(z) * (-1.0), axis=1, keepdims=True)
    dp = c0 / z + dz
    ddl = dp * np.exp(a * 0.5) / np.square(np.square(dl) * f64(sharp) + 1.0) * (-1.0) * f64(sharp) * dl * 2.0
    da = dp / (np.square(dl) * f64(sharp) + 1.0) * np.exp(a * 0.5) * 0.5 + ddl
    gs = da * 512.0
    gf = np.zeros((Q, T))
    gf[:, idx] = gs
    y = f64(old) + gf
    return y

@@ -1,0 +1,178 @@
+from contextlib import ExitStack
+
+import concourse.mybir as mybir
+
+D, E, T, I, Q = 512, 512, 2048, 512, 128
+FLOPS = 3 * 2 * 512 * Q * I
+
+F32 = mybir.dt.float32
+BF16 = mybir.dt.bfloat16
+I32 = mybir.dt.int32
+U32 = mybir.dt.uint32
+U16 = mybir.dt.uint16
+U8 = mybir.dt.uint8
+FP8X4 = mybir.dt.float8_e4m3fn_x4
+FP4X4 = mybir.dt.float4_e2m1fn_x4
+ALU = mybir.AluOpType
+ACT = mybir.ActivationFunctionType
+
+P = 128
+PACK = 4
+HALF = I // 2
+OUT_CHUNKS = 4
+
+
+def tile_attend_balikescores_s_kernel(tc, query, query2, keys_words, keys_scales, sharp, gout,
+                                       vals_words, vals_scales, old, offs, out):
+    nc = tc.nc
+    with ExitStack() as ctx:
+        sb = ctx.enter_context(tc.tile_pool(name="sb", bufs=1))
+        ps = ctx.enter_context(tc.psum_pool(name="ps", bufs=1))
+
+        def load_rows(queue, name, rows, tag=None):
+            raw = sb.tile([P, PACK, Q], F32, name=name, tag=tag or name)
+            queue.dma_start(out=raw[:], in_=rows.rearrange("(p j) w -> p j w", j=PACK))
+            return raw
+
+        def load_words(queue, name, words, tag=None):
+            pool_words = sb.tile([P, T], U16, name=name, tag=tag or name)
+            queue.dma_start(out=pool_words[:].bitcast(I32), in_=words[0].bitcast(I32))
+            return pool_words
+
+        def load_scale_rows(queue, plane, scales):
+            for quad in range(4):
+                queue.dma_start(out=plane[32 * quad:32 * quad + 4, :].bitcast(I32),
+                                in_=scales[0][4 * quad:4 * quad + 4, :].bitcast(I32))
+
+        def quantise(name, raws, signs, tag=None):
+            n = len(raws)
+            grouped = sb.tile([P, n * Q, PACK], BF16, name=name + "_grouped", tag=name + "_grouped", align_bytes=64)
+            for k, raw in enumerate(raws):
+                nc.scalar.activation(out=grouped[:, k * Q:(k + 1) * Q, :], in_=raw[:].rearrange("p j w -> p w j"),
+                                     func=ACT.Copy, scale=signs[k])
+            codes = sb.tile([P, n * Q], U32, name=name + "_codes", tag=tag or name + "_codes", align_bytes=64)
+            scales = sb.tile([P, n * Q], U8, name=name + "_scales", align_bytes=64)
+            nc.vector.quantize_mx(out=codes[:].bitcast(FP8X4), scales=scales[:],
+                                  in_=grouped[:].rearrange("p w j -> p (w j)"))
+            return [(codes[:, k * Q:(k + 1) * Q], scales[:, k * Q:(k + 1) * Q]) for k in range(n)]
+
+        def gather(name, window, dtype, first, count, tag=None):
+            picked = sb.tile([P, count], dtype, name=name, tag=tag or name, align_bytes=64)
+            nc.vector.tensor_copy(picked[:], window[:].indirect(offsets[:, first // 16:(first + count) // 16]))
+            return picked
+
+        def product(name, rows, words, scales, count):
+            acc = ps.tile([P, count], F32, name=name)
+            nc.tensor.matmul_mx(out=acc[:], lhsT=rows[0].bitcast(FP8X4), lhsT_scale=rows[1],
+                                rhs=words.bitcast(FP4X4), rhs_scale=scales, start=True, stop=True)
+            return acc
+
+        def row(name, tag=None):
+            return sb.tile([P, I], F32, name=name, tag=tag or name)
+
+        def col(name):
+            return sb.tile([P, 1], F32, name=name)
+
+        offsets = sb.tile([P, I // 16], U16, name="offsets")
+        nc.sync.dma_start(offsets[:], offs)
+        raw_q = load_rows(nc.scalar, "raw_q", query)
+        raw_q2 = load_rows(nc.scalar, "raw_q2", query2)
+        key_words = load_words(nc.scalar, "key_words", keys_words)
+
+        key_bytes = sb.tile([P, T], U8, name="key_bytes", tag="key_bytes", align_bytes=64)
+        nc.vector.memset(key_bytes[:].bitcast(I32), 0)
+        load_scale_rows(nc.sync, key_bytes, keys_scales)
+        warm = sb.tile([P, 8], F32, name="warm", tag="warm")
+        nc.gpsimd.memset(warm[:], 1.0)
+        warm_out = sb.tile([P, 8], F32, name="warm_out", tag="warm_out")
+        nc.scalar.activation(out=warm_out[:], in_=warm[:], func=ACT.Ln)
+
+        window = sb.tile([P, T], F32, name="window")
+        nc.vector.memset(window[:], 0.0)
+        val_bytes = sb.tile([P, T], U8, name="val_bytes", tag="val_bytes")
+        nc.vector.memset(val_bytes[:].bitcast(I32), 0)
+
+        sharp_col = col("sharp_col")
+        nc.gpsimd.dma_start(out=sharp_col[:], in_=sharp)
+        val_words = load_words(nc.sync, "val_words", vals_words, tag="warm")
+        raw_g = load_rows(nc.sync, "raw_g", gout, tag="warm_out")
+        load_scale_rows(nc.sync, val_bytes, vals_scales)
+
+        key_bytes_g = gather("key_bytes_g", key_bytes, U8, 0, I)
+        q, neg_q2 = quantise("q", [raw_q, raw_q2], [1.0, -1.0], tag="key_bytes")
+        old_sb = sb.tile([P, T], F32, name="old_sb", tag="raw_q2")
+        nc.sync.dma_start(out=old_sb[:], in_=old)
+        terms = sb.tile([P, 2], F32, name="terms")
+        nc.gpsimd.tensor_scalar(terms[:, 0:1], sharp_col[:], 1024.0, 0.0, ALU.mult, ALU.add)
+        nc.gpsimd.memset(terms[:, 1:2], -256.0)
+
+        key_words_g = sb.tile([P, I], U16, name="key_words_g", tag="q_grouped", align_bytes=64)
+        lo, hi = slice(0, HALF), slice(HALF, I)
+        nc.vector.tensor_copy(key_words_g[:, lo], key_words[:].indirect(offsets[:, 0:HALF // 16]))
+        a_lo = product("a_lo", q, key_words_g[:, lo], key_bytes_g[:, lo], HALF)
+        neg_b_lo = product("neg_b_lo", neg_q2, key_words_g[:, lo], key_bytes_g[:, lo], HALF)
+        nc.vector.tensor_copy(key_words_g[:, hi], key_words[:].indirect(offsets[:, HALF // 16:I // 16]))
+        dl_hi = ps.tile([P, HALF], F32, name="dl_hi")
+        for k in range(HALF // P):
+            cols = slice(HALF + k * P, HALF + (k + 1) * P)
+            for first, rows in ((True, neg_q2), (False, q)):
+                nc.tensor.matmul_mx(out=dl_hi[:, k * P:(k + 1) * P], lhsT=rows[0].bitcast(FP8X4), lhsT_scale=rows[1],
+                                    rhs=key_words_g[:, cols].bitcast(FP4X4), rhs_scale=key_bytes_g[:, cols],
+                                    start=first, stop=not first)
+        a_hi = product("a_hi", q, key_words_g[:, hi], key_bytes_g[:, hi], HALF)
+
+        def half(name, tag=None):
+            return sb.tile([P, HALF], F32, name=name, tag=tag or name, align_bytes=64)
+
+        neg_half_lo = half("neg_half_lo")
+        lowest_lo = col("lowest_lo")
+        nc.vector.tensor_scalar(neg_half_lo[:], a_lo[:], -0.5, None, ALU.mult, ALU.min, accum_out=lowest_lo[:])
+        dl_lo = half("dl_lo")
+        nc.vector.scalar_tensor_tensor(dl_lo[:], neg_half_lo[:], -2.0, neg_b_lo[:], ALU.mult, ALU.add)
+        log_u = row("log_u")
+        for name, dl, cols in (("sq_lo", dl_lo, lo), ("sq_hi", dl_hi, hi)):
+            sq = half(name)
+            nc.scalar.activation(out=sq[:], in_=dl[:], func=ACT.Square)
+            nc.scalar.activation(out=log_u[:, cols], in_=sq[:], func=ACT.Ln, scale=sharp_col[:], bias=1.0)
+        r = row("r", tag="warm_out")
+        nc.scalar.activation(out=r[:, I - 32:I], in_=log_u[:, I - 32:I], func=ACT.Exp, scale=-1.0)
+
+        val_words_g = gather("val_words_g", val_words, U16, 0, I, tag="neg_half_lo")
+        neg_half_hi = half("neg_half_hi")
+        shift = col("shift")
+        nc.vector.tensor_scalar(neg_half_hi[:], a_hi[:], -0.5, lowest_lo[:], ALU.mult, ALU.min, accum_out=shift[:])
+        neg_log_p = row("neg_log_p")
+        nc.vector.scalar_tensor_tensor(neg_log_p[:, lo], a_lo[:], -0.5, log_u[:, lo], ALU.mult, ALU.add)
+        nc.vector.tensor_tensor(neg_log_p[:, hi], log_u[:, hi], neg_half_hi[:], ALU.add)
+        p = row("p")
+        z = col("z")
+        nc.scalar.activation(out=p[:], in_=neg_log_p[:], func=ACT.Exp, scale=-1.0, bias=shift[:], accum_out=z[:])
+        nc.scalar.activation(out=r[:, 0:I - 32], in_=log_u[:, 0:I - 32], func=ACT.Exp, scale=-1.0)
+
+        (g,) = quantise("g", [raw_g], [1.0])
+        val_bytes_g = gather("val_bytes_g", val_bytes, U8, 0, I, tag="sq_hi")
+        c0 = product("c0", g, val_words_g[:], val_bytes_g[:], I)
+
+        rz = sb.tile([P, 1], F32, name="rz", tag="val_bytes")
+        nc.vector.reciprocal(rz[:], z[:])
+        scaled = sb.tile([P, 2], F32, name="scaled")
+        nc.vector.tensor_scalar(scaled[:], terms[:], rz[:], None, ALU.mult)
+        tilt = row("tilt")
+        for dl, cols in ((dl_lo, lo), (dl_hi, hi)):
+            nc.vector.scalar_tensor_tensor(tilt[:, cols], dl[:], scaled[:, 0:1], r[:, cols], ALU.mult, ALU.mult)
+        cp = sb.tile([P, I], F32, name="cp", tag="dl_lo", align_bytes=64)
+        mean = col("mean")
+        nc.vector.scalar_tensor_tensor(cp[:], c0[:], rz[:], p[:], ALU.mult, ALU.mult, accum_out=mean[:])
+        dp = row("dp")
+        nc.scalar.activation(out=dp[:], in_=c0[:], func=ACT.Identity, scale=-1.0, bias=mean[:])
+        w = row("w")
+        nc.vector.scalar_tensor_tensor(w[:], tilt[:], scaled[:, 1:2], p[:], ALU.add, ALU.mult)
+
+        nc.vector.tensor_tensor(window[:].indirect(offsets[:]), dp[:], w[:], ALU.mult)
+
+        width = T // OUT_CHUNKS
+        for c in range(OUT_CHUNKS):
+            cols = slice(c * width, (c + 1) * width)
+            total = sb.tile([P, width], F32, name="total%d" % c)
+            nc.vector.tensor_tensor(total[:], window[:, cols], old_sb[:, cols], ALU.add)
+            nc.sync.dma_start(out=out[:, cols], in_=total[:])

@@ -30,7 +30,7 @@ def tile_attend_balikescores_s_kernel(tc, query, query2, keys_words, keys_scales
         ps = ctx.enter_context(tc.psum_pool(name="ps", bufs=1))
 
         def load_rows(queue, name, rows, tag=None):
-            raw = sb.tile([P, PACK, Q], F32, name=name, tag=tag or name)
+            raw = sb.tile([P, PACK, Q], F32, name=name, tag=tag or name, align_bytes=64)
             queue.dma_start(out=raw[:], in_=rows.rearrange("(p j) w -> p j w", j=PACK))
             return raw
 
@@ -48,7 +48,8 @@ def tile_attend_balikescores_s_kernel(tc, query, query2, keys_words, keys_scales
             n = len(raws)
             grouped = sb.tile([P, n * Q, PACK], BF16, name=name + "_grouped", tag=name + "_grouped", align_bytes=64)
             for k, raw in enumerate(raws):
-                nc.scalar.activation(out=grouped[:, k * Q:(k + 1) * Q, :], in_=raw[:].rearrange("p j w -> p w j"),
+                nc.scalar.activation(out=grouped[:, k * Q:(k + 1) * Q, :].rearrange("p (c i) j -> p c j i", i=4),
+                                     in_=raw[:].rearrange("p j (c i) -> p c j i", i=4),
                                      func=ACT.Copy, scale=signs[k])
             codes = sb.tile([P, n * Q], U32, name=name + "_codes", tag=tag or name + "_codes", align_bytes=64)
             scales = sb.tile([P, n * Q], U8, name=name + "_scales", align_bytes=64)
@@ -61,11 +62,9 @@ def tile_attend_balikescores_s_kernel(tc, query, query2, keys_words, keys_scales
             nc.vector.tensor_copy(picked[:], window[:].indirect(offsets[:, first // 16:(first + count) // 16]))
             return picked
 
-        def product(name, rows, words, scales, count):
-            acc = ps.tile([P, count], F32, name=name)
-            nc.tensor.matmul_mx(out=acc[:], lhsT=rows[0].bitcast(FP8X4), lhsT_scale=rows[1],
-                                rhs=words.bitcast(FP4X4), rhs_scale=scales, start=True, stop=True)
-            return acc
+        def product(acc, rows, words, scales, start=True, stop=True):
+            nc.tensor.matmul_mx(out=acc, lhsT=rows[0].bitcast(FP8X4), lhsT_scale=rows[1],
+                                rhs=words.bitcast(FP4X4), rhs_scale=scales, start=start, stop=stop)
 
         def row(name, tag=None):
             return sb.tile([P, I], F32, name=name, tag=tag or name)
@@ -73,100 +72,93 @@ def tile_attend_balikescores_s_kernel(tc, query, query2, keys_words, keys_scales
         def col(name):
             return sb.tile([P, 1], F32, name=name)
 
-        offsets = sb.tile([P, I // 16], U16, name="offsets")
-        nc.sync.dma_start(offsets[:], offs)
-        raw_q = load_rows(nc.scalar, "raw_q", query)
-        raw_q2 = load_rows(nc.scalar, "raw_q2", query2)
-        key_words = load_words(nc.scalar, "key_words", keys_words)
-
         key_bytes = sb.tile([P, T], U8, name="key_bytes", tag="key_bytes", align_bytes=64)
-        nc.vector.memset(key_bytes[:].bitcast(I32), 0)
-        load_scale_rows(nc.sync, key_bytes, keys_scales)
+        nc.vector.memset(key_bytes[:, 0:T // 2].bitcast(I32), 0)
+        nc.gpsimd.memset(key_bytes[:, T // 2:T].bitcast(I32), 0)
         warm = sb.tile([P, 8], F32, name="warm", tag="warm")
-        nc.gpsimd.memset(warm[:], 1.0)
-        warm_out = sb.tile([P, 8], F32, name="warm_out", tag="warm_out")
+        nc.vector.memset(warm[:], 1.0)
+        warm_out = sb.tile([P, 8], F32, name="warm_out", tag="warm_out", align_bytes=64)
         nc.scalar.activation(out=warm_out[:], in_=warm[:], func=ACT.Ln)
-
         window = sb.tile([P, T], F32, name="window")
         nc.vector.memset(window[:], 0.0)
         val_bytes = sb.tile([P, T], U8, name="val_bytes", tag="val_bytes")
         nc.vector.memset(val_bytes[:].bitcast(I32), 0)
 
+        offsets = sb.tile([P, I // 16], U16, name="offsets")
+        nc.sync.dma_start(offsets[:], offs)
+        raw_q2 = load_rows(nc.sync, "raw_q2", query2)
         sharp_col = col("sharp_col")
-        nc.gpsimd.dma_start(out=sharp_col[:], in_=sharp)
-        val_words = load_words(nc.sync, "val_words", vals_words, tag="warm")
+        nc.sync.dma_start(out=sharp_col[:], in_=sharp)
+        load_scale_rows(nc.sync, key_bytes, keys_scales)
+        raw_q = load_rows(nc.sync, "raw_q", query)
+        key_words = load_words(nc.sync, "key_words", keys_words)
         raw_g = load_rows(nc.sync, "raw_g", gout, tag="warm_out")
+        val_words = load_words(nc.sync, "val_words", vals_words, tag="warm")
         load_scale_rows(nc.sync, val_bytes, vals_scales)
 
         key_bytes_g = gather("key_bytes_g", key_bytes, U8, 0, I)
-        q, neg_q2 = quantise("q", [raw_q, raw_q2], [1.0, -1.0], tag="key_bytes")
-        old_sb = sb.tile([P, T], F32, name="old_sb", tag="raw_q2")
+        neg_q2, q = quantise("q", [raw_q2, raw_q], [-1.0, 1.0], tag="key_bytes")
+        old_sb = sb.tile([P, T], F32, name="old_sb", tag="raw_q", align_bytes=64)
         nc.sync.dma_start(out=old_sb[:], in_=old)
-        terms = sb.tile([P, 2], F32, name="terms")
-        nc.gpsimd.tensor_scalar(terms[:, 0:1], sharp_col[:], 1024.0, 0.0, ALU.mult, ALU.add)
-        nc.gpsimd.memset(terms[:, 1:2], -256.0)
+        (g,) = quantise("g", [raw_g], [1024.0])
 
         key_words_g = sb.tile([P, I], U16, name="key_words_g", tag="q_grouped", align_bytes=64)
         lo, hi = slice(0, HALF), slice(HALF, I)
         nc.vector.tensor_copy(key_words_g[:, lo], key_words[:].indirect(offsets[:, 0:HALF // 16]))
-        a_lo = product("a_lo", q, key_words_g[:, lo], key_bytes_g[:, lo], HALF)
-        neg_b_lo = product("neg_b_lo", neg_q2, key_words_g[:, lo], key_bytes_g[:, lo], HALF)
-        nc.vector.tensor_copy(key_words_g[:, hi], key_words[:].indirect(offsets[:, HALF // 16:I // 16]))
+        a_lo = ps.tile([P, HALF], F32, name="a_lo")
+        neg_b_lo = ps.tile([P, HALF], F32, name="neg_b_lo")
         dl_hi = ps.tile([P, HALF], F32, name="dl_hi")
+        a_hi = ps.tile([P, HALF], F32, name="a_hi")
+        product(a_lo[:], q, key_words_g[:, lo], key_bytes_g[:, lo])
+        product(neg_b_lo[:], neg_q2, key_words_g[:, lo], key_bytes_g[:, lo])
+        nc.vector.tensor_copy(key_words_g[:, hi], key_words[:].indirect(offsets[:, HALF // 16:I // 16]))
         for k in range(HALF // P):
             cols = slice(HALF + k * P, HALF + (k + 1) * P)
-            for first, rows in ((True, neg_q2), (False, q)):
-                nc.tensor.matmul_mx(out=dl_hi[:, k * P:(k + 1) * P], lhsT=rows[0].bitcast(FP8X4), lhsT_scale=rows[1],
-                                    rhs=key_words_g[:, cols].bitcast(FP4X4), rhs_scale=key_bytes_g[:, cols],
-                                    start=first, stop=not first)
-        a_hi = product("a_hi", q, key_words_g[:, hi], key_bytes_g[:, hi], HALF)
+            product(dl_hi[:, k * P:(k + 1) * P], neg_q2, key_words_g[:, cols], key_bytes_g[:, cols], stop=False)
+            product(dl_hi[:, k * P:(k + 1) * P], q, key_words_g[:, cols], key_bytes_g[:, cols], start=False)
+        product(a_hi[:], q, key_words_g[:, hi], key_bytes_g[:, hi])
 
-        def half(name, tag=None):
-            return sb.tile([P, HALF], F32, name=name, tag=tag or name, align_bytes=64)
-
-        neg_half_lo = half("neg_half_lo")
+        neg_half = row("neg_half")
         lowest_lo = col("lowest_lo")
-        nc.vector.tensor_scalar(neg_half_lo[:], a_lo[:], -0.5, None, ALU.mult, ALU.min, accum_out=lowest_lo[:])
-        dl_lo = half("dl_lo")
-        nc.vector.scalar_tensor_tensor(dl_lo[:], neg_half_lo[:], -2.0, neg_b_lo[:], ALU.mult, ALU.add)
+        nc.vector.tensor_scalar(neg_half[:, lo], a_lo[:], -0.5, None, ALU.mult, ALU.min, accum_out=lowest_lo[:])
+        dl_lo = sb.tile([P, HALF], F32, name="dl_lo")
+        nc.vector.scalar_tensor_tensor(dl_lo[:], neg_half[:, lo], -2.0, neg_b_lo[:], ALU.mult, ALU.add)
+        sq = sb.tile([P, I], F32, name="sq", tag="warm_out", align_bytes=64)
         log_u = row("log_u")
-        for name, dl, cols in (("sq_lo", dl_lo, lo), ("sq_hi", dl_hi, hi)):
-            sq = half(name)
-            nc.scalar.activation(out=sq[:], in_=dl[:], func=ACT.Square)
-            nc.scalar.activation(out=log_u[:, cols], in_=sq[:], func=ACT.Ln, scale=sharp_col[:], bias=1.0)
-        r = row("r", tag="warm_out")
-        nc.scalar.activation(out=r[:, I - 32:I], in_=log_u[:, I - 32:I], func=ACT.Exp, scale=-1.0)
+        for dl, cols in ((dl_hi, hi), (dl_lo, lo)):
+            nc.scalar.activation(out=sq[:, cols], in_=dl[:], func=ACT.Square)
+        for cols in (hi, lo):
+            nc.scalar.activation(out=log_u[:, cols], in_=sq[:, cols], func=ACT.Ln, scale=sharp_col[:], bias=1.0)
+        r = row("r")
+        nc.scalar.activation(out=r[:], in_=log_u[:], func=ACT.Exp, scale=-1.0)
 
-        val_words_g = gather("val_words_g", val_words, U16, 0, I, tag="neg_half_lo")
-        neg_half_hi = half("neg_half_hi")
+        val_words_g = gather("val_words_g", val_words, U16, 0, I, tag="q_grouped")
         shift = col("shift")
-        nc.vector.tensor_scalar(neg_half_hi[:], a_hi[:], -0.5, lowest_lo[:], ALU.mult, ALU.min, accum_out=shift[:])
+        nc.vector.tensor_scalar(neg_half[:, hi], a_hi[:], -0.5, lowest_lo[:], ALU.mult, ALU.min, accum_out=shift[:])
+        val_bytes_g = gather("val_bytes_g", val_bytes, U8, 0, I, tag="key_bytes_g")
+        c0 = ps.tile([P, I], F32, name="c0")
+        product(c0[:], g, val_words_g[:], val_bytes_g[:])
+
         neg_log_p = row("neg_log_p")
-        nc.vector.scalar_tensor_tensor(neg_log_p[:, lo], a_lo[:], -0.5, log_u[:, lo], ALU.mult, ALU.add)
-        nc.vector.tensor_tensor(neg_log_p[:, hi], log_u[:, hi], neg_half_hi[:], ALU.add)
+        nc.vector.tensor_tensor(neg_log_p[:], log_u[:], neg_half[:], ALU.add)
         p = row("p")
         z = col("z")
         nc.scalar.activation(out=p[:], in_=neg_log_p[:], func=ACT.Exp, scale=-1.0, bias=shift[:], accum_out=z[:])
-        nc.scalar.activation(out=r[:, 0:I - 32], in_=log_u[:, 0:I - 32], func=ACT.Exp, scale=-1.0)
 
-        (g,) = quantise("g", [raw_g], [1.0])
-        val_bytes_g = gather("val_bytes_g", val_bytes, U8, 0, I, tag="sq_hi")
-        c0 = product("c0", g, val_words_g[:], val_bytes_g[:], I)
-
-        rz = sb.tile([P, 1], F32, name="rz", tag="val_bytes")
-        nc.vector.reciprocal(rz[:], z[:])
-        scaled = sb.tile([P, 2], F32, name="scaled")
-        nc.vector.tensor_scalar(scaled[:], terms[:], rz[:], None, ALU.mult)
-        tilt = row("tilt")
+        tilt = row("tilt", tag="val_bytes")
         for dl, cols in ((dl_lo, lo), (dl_hi, hi)):
-            nc.vector.scalar_tensor_tensor(tilt[:, cols], dl[:], scaled[:, 0:1], r[:, cols], ALU.mult, ALU.mult)
-        cp = sb.tile([P, I], F32, name="cp", tag="dl_lo", align_bytes=64)
+            nc.vector.scalar_tensor_tensor(tilt[:, cols], dl[:], sharp_col[:], r[:, cols], ALU.mult, ALU.mult)
+        rz = col("rz")
+        nc.vector.reciprocal(rz[:], z[:])
+        cp = row("cp")
         mean = col("mean")
         nc.vector.scalar_tensor_tensor(cp[:], c0[:], rz[:], p[:], ALU.mult, ALU.mult, accum_out=mean[:])
+        weight = row("weight")
+        nc.scalar.activation(out=weight[:], in_=p[:], func=ACT.Copy, scale=rz[:])
         dp = row("dp")
         nc.scalar.activation(out=dp[:], in_=c0[:], func=ACT.Identity, scale=-1.0, bias=mean[:])
         w = row("w")
-        nc.vector.scalar_tensor_tensor(w[:], tilt[:], scaled[:, 1:2], p[:], ALU.add, ALU.mult)
+        nc.vector.scalar_tensor_tensor(w[:], tilt[:], -0.25, weight[:], ALU.add, ALU.mult)
 
         nc.vector.tensor_tensor(window[:].indirect(offsets[:]), dp[:], w[:], ALU.mult)
 

@@ -19,7 +19,7 @@ ACT = mybir.ActivationFunctionType
 P = 128
 PACK = 4
 HALF = I // 2
-OUT_CHUNKS = 4
+OUT_EDGES = (0, 256, 768, 1280, 1792, 2048)
 
 
 def tile_attend_balikescores_s_kernel(tc, query, query2, keys_words, keys_scales, sharp, gout,
@@ -27,6 +27,7 @@ def tile_attend_balikescores_s_kernel(tc, query, query2, keys_words, keys_scales
     nc = tc.nc
     with ExitStack() as ctx:
         sb = ctx.enter_context(tc.tile_pool(name="sb", bufs=1))
+        reuse = ctx.enter_context(tc.tile_pool(name="reuse", bufs=1))
         ps = ctx.enter_context(tc.psum_pool(name="ps", bufs=1))
 
         def load_rows(queue, name, rows, tag=None):
@@ -40,18 +41,16 @@ def tile_attend_balikescores_s_kernel(tc, query, query2, keys_words, keys_scales
             return pool_words
 
         def load_scale_rows(queue, plane, scales):
-            for quad in range(4):
-                queue.dma_start(out=plane[32 * quad:32 * quad + 4, :].bitcast(I32),
-                                in_=scales[0][4 * quad:4 * quad + 4, :].bitcast(I32))
+            for r in range(4):
+                queue.dma_start(out=plane[r:P:32, :].bitcast(I32), in_=scales[0][r:16:4, :].bitcast(I32))
 
-        def quantise(name, raws, signs, tag=None):
+        def quantise(name, raws, signs, codes):
             n = len(raws)
             grouped = sb.tile([P, n * Q, PACK], BF16, name=name + "_grouped", tag=name + "_grouped", align_bytes=64)
             for k, raw in enumerate(raws):
                 nc.scalar.activation(out=grouped[:, k * Q:(k + 1) * Q, :].rearrange("p (c i) j -> p c j i", i=4),
                                      in_=raw[:].rearrange("p j (c i) -> p c j i", i=4),
                                      func=ACT.Copy, scale=signs[k])
-            codes = sb.tile([P, n * Q], U32, name=name + "_codes", tag=tag or name + "_codes", align_bytes=64)
             scales = sb.tile([P, n * Q], U8, name=name + "_scales", align_bytes=64)
             nc.vector.quantize_mx(out=codes[:].bitcast(FP8X4), scales=scales[:],
                                   in_=grouped[:].rearrange("p w j -> p (w j)"))
@@ -72,7 +71,7 @@ def tile_attend_balikescores_s_kernel(tc, query, query2, keys_words, keys_scales
         def col(name):
             return sb.tile([P, 1], F32, name=name)
 
-        key_bytes = sb.tile([P, T], U8, name="key_bytes", tag="key_bytes", align_bytes=64)
+        key_bytes = reuse.tile([P, T], U8, name="key_bytes", align_bytes=64, offset=0)
         nc.vector.memset(key_bytes[:, 0:T // 2].bitcast(I32), 0)
         nc.gpsimd.memset(key_bytes[:, T // 2:T].bitcast(I32), 0)
         warm = sb.tile([P, 8], F32, name="warm", tag="warm")
@@ -87,8 +86,6 @@ def tile_attend_balikescores_s_kernel(tc, query, query2, keys_words, keys_scales
         offsets = sb.tile([P, I // 16], U16, name="offsets")
         nc.sync.dma_start(offsets[:], offs)
         raw_q2 = load_rows(nc.sync, "raw_q2", query2)
-        sharp_col = col("sharp_col")
-        nc.sync.dma_start(out=sharp_col[:], in_=sharp)
         load_scale_rows(nc.sync, key_bytes, keys_scales)
         raw_q = load_rows(nc.sync, "raw_q", query)
         key_words = load_words(nc.sync, "key_words", keys_words)
@@ -97,12 +94,16 @@ def tile_attend_balikescores_s_kernel(tc, query, query2, keys_words, keys_scales
         load_scale_rows(nc.sync, val_bytes, vals_scales)
 
         key_bytes_g = gather("key_bytes_g", key_bytes, U8, 0, I)
-        neg_q2, q = quantise("q", [raw_q2, raw_q], [-1.0, 1.0], tag="key_bytes")
+        q_codes = reuse.tile([P, 2 * Q], U32, name="q_codes", align_bytes=64, offset=0)
+        neg_q2, q = quantise("q", [raw_q2, raw_q], [-1.0, 1.0], q_codes)
+        sharp_col = sb.tile([P, 1], F32, name="sharp_col", tag="raw_q2", align_bytes=64)
+        nc.sync.dma_start(out=sharp_col[:], in_=sharp)
         old_sb = sb.tile([P, T], F32, name="old_sb", tag="raw_q", align_bytes=64)
         nc.sync.dma_start(out=old_sb[:], in_=old)
-        (g,) = quantise("g", [raw_g], [1024.0])
+        g_codes = sb.tile([P, Q], U32, name="g_codes", align_bytes=64)
+        (g,) = quantise("g", [raw_g], [1024.0], g_codes)
 
-        key_words_g = sb.tile([P, I], U16, name="key_words_g", tag="q_grouped", align_bytes=64)
+        key_words_g = reuse.tile([P, I], U16, name="key_words_g", align_bytes=64, offset=T // 2)
         lo, hi = slice(0, HALF), slice(HALF, I)
         nc.vector.tensor_copy(key_words_g[:, lo], key_words[:].indirect(offsets[:, 0:HALF // 16]))
         a_lo = ps.tile([P, HALF], F32, name="a_lo")
@@ -132,7 +133,8 @@ def tile_attend_balikescores_s_kernel(tc, query, query2, keys_words, keys_scales
         r = row("r")
         nc.scalar.activation(out=r[:], in_=log_u[:], func=ACT.Exp, scale=-1.0)
 
-        val_words_g = gather("val_words_g", val_words, U16, 0, I, tag="q_grouped")
+        val_words_g = reuse.tile([P, I], U16, name="val_words_g", align_bytes=64, offset=T // 2)
+        nc.vector.tensor_copy(val_words_g[:], val_words[:].indirect(offsets[:]))
         shift = col("shift")
         nc.vector.tensor_scalar(neg_half[:, hi], a_hi[:], -0.5, lowest_lo[:], ALU.mult, ALU.min, accum_out=shift[:])
         val_bytes_g = gather("val_bytes_g", val_bytes, U8, 0, I, tag="key_bytes_g")
@@ -162,9 +164,8 @@ def tile_attend_balikescores_s_kernel(tc, query, query2, keys_words, keys_scales
 
         nc.vector.tensor_tensor(window[:].indirect(offsets[:]), dp[:], w[:], ALU.mult)
 
-        width = T // OUT_CHUNKS
-        for c in range(OUT_CHUNKS):
-            cols = slice(c * width, (c + 1) * width)
-            total = sb.tile([P, width], F32, name="total%d" % c)
+        for c in range(len(OUT_EDGES) - 1):
+            cols = slice(OUT_EDGES[c], OUT_EDGES[c + 1])
+            total = sb.tile([P, cols.stop - cols.start], F32, name="total%d" % c)
             nc.vector.tensor_tensor(total[:], window[:, cols], old_sb[:, cols], ALU.add)
             nc.sync.dma_start(out=out[:, cols], in_=total[:])

@@ -131,30 +131,33 @@ def tile_attend_balikescores_s_kernel(tc, query, query2, keys_words, keys_scales
         for cols in (hi, lo):
             nc.scalar.activation(out=log_u[:, cols], in_=sq[:, cols], func=ACT.Ln, scale=sharp_col[:], bias=1.0)
         r = row("r")
-        nc.scalar.activation(out=r[:], in_=log_u[:], func=ACT.Exp, scale=-1.0)
+        nc.scalar.activation(out=r[:, hi], in_=log_u[:, hi], func=ACT.Exp, scale=-1.0)
 
-        val_words_g = reuse.tile([P, I], U16, name="val_words_g", align_bytes=64, offset=T // 2)
-        nc.vector.tensor_copy(val_words_g[:], val_words[:].indirect(offsets[:]))
         shift = col("shift")
         nc.vector.tensor_scalar(neg_half[:, hi], a_hi[:], -0.5, lowest_lo[:], ALU.mult, ALU.min, accum_out=shift[:])
-        val_bytes_g = gather("val_bytes_g", val_bytes, U8, 0, I, tag="key_bytes_g")
+        val_words_g = reuse.tile([P, I], U16, name="val_words_g", align_bytes=64, offset=T // 2)
+        nc.vector.tensor_copy(val_words_g[:], val_words[:].indirect(offsets[:]))
+        val_bytes_g = sb.tile([P, I], U8, name="val_bytes_g", tag="key_bytes_g", align_bytes=64)
         c0 = ps.tile([P, I], F32, name="c0")
-        product(c0[:], g, val_words_g[:], val_bytes_g[:])
+        for cols in (lo, hi):
+            nc.vector.tensor_copy(val_bytes_g[:, cols], val_bytes[:].indirect(offsets[:, cols.start // 16:cols.stop // 16]))
+            product(c0[:, cols], g, val_words_g[:, cols], val_bytes_g[:, cols])
 
         neg_log_p = row("neg_log_p")
-        nc.vector.tensor_tensor(neg_log_p[:], log_u[:], neg_half[:], ALU.add)
+        nc.gpsimd.tensor_tensor(neg_log_p[:], log_u[:], neg_half[:], ALU.add)
         p = row("p")
         z = col("z")
         nc.scalar.activation(out=p[:], in_=neg_log_p[:], func=ACT.Exp, scale=-1.0, bias=shift[:], accum_out=z[:])
+        nc.scalar.activation(out=r[:, lo], in_=log_u[:, lo], func=ACT.Exp, scale=-1.0)
 
         tilt = row("tilt", tag="val_bytes")
-        for dl, cols in ((dl_lo, lo), (dl_hi, hi)):
-            nc.vector.scalar_tensor_tensor(tilt[:, cols], dl[:], sharp_col[:], r[:, cols], ALU.mult, ALU.mult)
+        nc.vector.scalar_tensor_tensor(tilt[:, hi], dl_hi[:], sharp_col[:], r[:, hi], ALU.mult, ALU.mult)
         rz = col("rz")
         nc.vector.reciprocal(rz[:], z[:])
         cp = row("cp")
         mean = col("mean")
         nc.vector.scalar_tensor_tensor(cp[:], c0[:], rz[:], p[:], ALU.mult, ALU.mult, accum_out=mean[:])
+        nc.vector.scalar_tensor_tensor(tilt[:, lo], dl_lo[:], sharp_col[:], r[:, lo], ALU.mult, ALU.mult)
         weight = row("weight")
         nc.scalar.activation(out=weight[:], in_=p[:], func=ACT.Copy, scale=rz[:])
         dp = row("dp")

from contextlib import ExitStack

import concourse.mybir as mybir

D, E, T, I, Q = 512, 512, 2048, 512, 128
FLOPS = 3 * 2 * 512 * Q * I

F32 = mybir.dt.float32
BF16 = mybir.dt.bfloat16
I32 = mybir.dt.int32
U32 = mybir.dt.uint32
U16 = mybir.dt.uint16
U8 = mybir.dt.uint8
FP8X4 = mybir.dt.float8_e4m3fn_x4
FP4X4 = mybir.dt.float4_e2m1fn_x4
ALU = mybir.AluOpType
ACT = mybir.ActivationFunctionType

P = 128
PACK = 4
HALF = I // 2
OUT_EDGES = (0, 256, 768, 1280, 1792, 2048)


def tile_attend_balikescores_s_kernel(tc, query, query2, keys_words, keys_scales, sharp, gout,
                                       vals_words, vals_scales, old, offs, out):
    nc = tc.nc
    with ExitStack() as ctx:
        sb = ctx.enter_context(tc.tile_pool(name="sb", bufs=1))
        reuse = ctx.enter_context(tc.tile_pool(name="reuse", bufs=1))
        ps = ctx.enter_context(tc.psum_pool(name="ps", bufs=1))

        def load_rows(queue, name, rows, tag=None):
            raw = sb.tile([P, PACK, Q], F32, name=name, tag=tag or name, align_bytes=64)
            queue.dma_start(out=raw[:], in_=rows.rearrange("(p j) w -> p j w", j=PACK))
            return raw

        def load_words(queue, name, words, tag=None):
            pool_words = sb.tile([P, T], U16, name=name, tag=tag or name)
            queue.dma_start(out=pool_words[:].bitcast(I32), in_=words[0].bitcast(I32))
            return pool_words

        def load_scale_rows(queue, plane, scales):
            for r in range(4):
                queue.dma_start(out=plane[r:P:32, :].bitcast(I32), in_=scales[0][r:16:4, :].bitcast(I32))

        def quantise(name, raws, signs, codes):
            n = len(raws)
            grouped = sb.tile([P, n * Q, PACK], BF16, name=name + "_grouped", tag=name + "_grouped", align_bytes=64)
            for k, raw in enumerate(raws):
                nc.scalar.activation(out=grouped[:, k * Q:(k + 1) * Q, :].rearrange("p (c i) j -> p c j i", i=4),
                                     in_=raw[:].rearrange("p j (c i) -> p c j i", i=4),
                                     func=ACT.Copy, scale=signs[k])
            scales = sb.tile([P, n * Q], U8, name=name + "_scales", align_bytes=64)
            nc.vector.quantize_mx(out=codes[:].bitcast(FP8X4), scales=scales[:],
                                  in_=grouped[:].rearrange("p w j -> p (w j)"))
            return [(codes[:, k * Q:(k + 1) * Q], scales[:, k * Q:(k + 1) * Q]) for k in range(n)]

        def gather(name, window, dtype, first, count, tag=None):
            picked = sb.tile([P, count], dtype, name=name, tag=tag or name, align_bytes=64)
            nc.vector.tensor_copy(picked[:], window[:].indirect(offsets[:, first // 16:(first + count) // 16]))
            return picked

        def product(acc, rows, words, scales, start=True, stop=True):
            nc.tensor.matmul_mx(out=acc, lhsT=rows[0].bitcast(FP8X4), lhsT_scale=rows[1],
                                rhs=words.bitcast(FP4X4), rhs_scale=scales, start=start, stop=stop)

        def row(name, tag=None):
            return sb.tile([P, I], F32, name=name, tag=tag or name)

        def col(name):
            return sb.tile([P, 1], F32, name=name)

        key_bytes = reuse.tile([P, T], U8, name="key_bytes", align_bytes=64, offset=0)
        nc.vector.memset(key_bytes[:, 0:T // 2].bitcast(I32), 0)
        nc.gpsimd.memset(key_bytes[:, T // 2:T].bitcast(I32), 0)
        warm = sb.tile([P, 8], F32, name="warm", tag="warm")
        nc.vector.memset(warm[:], 1.0)
        warm_out = sb.tile([P, 8], F32, name="warm_out", tag="warm_out", align_bytes=64)
        nc.scalar.activation(out=warm_out[:], in_=warm[:], func=ACT.Ln)
        window = sb.tile([P, T], F32, name="window")
        nc.vector.memset(window[:], 0.0)
        val_bytes = sb.tile([P, T], U8, name="val_bytes", tag="val_bytes")
        nc.vector.memset(val_bytes[:].bitcast(I32), 0)

        offsets = sb.tile([P, I // 16], U16, name="offsets")
        nc.sync.dma_start(offsets[:], offs)
        raw_q2 = load_rows(nc.sync, "raw_q2", query2)
        load_scale_rows(nc.sync, key_bytes, keys_scales)
        raw_q = load_rows(nc.sync, "raw_q", query)
        key_words = load_words(nc.sync, "key_words", keys_words)
        raw_g = load_rows(nc.sync, "raw_g", gout, tag="warm_out")
        val_words = load_words(nc.sync, "val_words", vals_words, tag="warm")
        load_scale_rows(nc.sync, val_bytes, vals_scales)

        key_bytes_g = gather("key_bytes_g", key_bytes, U8, 0, I)
        q_codes = reuse.tile([P, 2 * Q], U32, name="q_codes", align_bytes=64, offset=0)
        neg_q2, q = quantise("q", [raw_q2, raw_q], [-1.0, 1.0], q_codes)
        sharp_col = sb.tile([P, 1], F32, name="sharp_col", tag="raw_q2", align_bytes=64)
        nc.sync.dma_start(out=sharp_col[:], in_=sharp)
        old_sb = sb.tile([P, T], F32, name="old_sb", tag="raw_q", align_bytes=64)
        nc.sync.dma_start(out=old_sb[:], in_=old)
        g_codes = sb.tile([P, Q], U32, name="g_codes", align_bytes=64)
        (g,) = quantise("g", [raw_g], [1024.0], g_codes)

        key_words_g = reuse.tile([P, I], U16, name="key_words_g", align_bytes=64, offset=T // 2)
        lo, hi = slice(0, HALF), slice(HALF, I)
        nc.vector.tensor_copy(key_words_g[:, lo], key_words[:].indirect(offsets[:, 0:HALF // 16]))
        a_lo = ps.tile([P, HALF], F32, name="a_lo")
        neg_b_lo = ps.tile([P, HALF], F32, name="neg_b_lo")
        dl_hi = ps.tile([P, HALF], F32, name="dl_hi")
        a_hi = ps.tile([P, HALF], F32, name="a_hi")
        product(a_lo[:], q, key_words_g[:, lo], key_bytes_g[:, lo])
        product(neg_b_lo[:], neg_q2, key_words_g[:, lo], key_bytes_g[:, lo])
        nc.vector.tensor_copy(key_words_g[:, hi], key_words[:].indirect(offsets[:, HALF // 16:I // 16]))
        for k in range(HALF // P):
            cols = slice(HALF + k * P, HALF + (k + 1) * P)
            product(dl_hi[:, k * P:(k + 1) * P], neg_q2, key_words_g[:, cols], key_bytes_g[:, cols], stop=False)
            product(dl_hi[:, k * P:(k + 1) * P], q, key_words_g[:, cols], key_bytes_g[:, cols], start=False)
        product(a_hi[:], q, key_words_g[:, hi], key_bytes_g[:, hi])

        neg_half = row("neg_half")
        lowest_lo = col("lowest_lo")
        nc.vector.tensor_scalar(neg_half[:, lo], a_lo[:], -0.5, None, ALU.mult, ALU.min, accum_out=lowest_lo[:])
        dl_lo = sb.tile([P, HALF], F32, name="dl_lo")
        nc.vector.scalar_tensor_tensor(dl_lo[:], neg_half[:, lo], -2.0, neg_b_lo[:], ALU.mult, ALU.add)
        sq = sb.tile([P, I], F32, name="sq", tag="warm_out", align_bytes=64)
        log_u = row("log_u")
        for dl, cols in ((dl_hi, hi), (dl_lo, lo)):
            nc.scalar.activation(out=sq[:, cols], in_=dl[:], func=ACT.Square)
        for cols in (hi, lo):
            nc.scalar.activation(out=log_u[:, cols], in_=sq[:, cols], func=ACT.Ln, scale=sharp_col[:], bias=1.0)
        r = row("r")
        nc.scalar.activation(out=r[:, hi], in_=log_u[:, hi], func=ACT.Exp, scale=-1.0)

        shift = col("shift")
        nc.vector.tensor_scalar(neg_half[:, hi], a_hi[:], -0.5, lowest_lo[:], ALU.mult, ALU.min, accum_out=shift[:])
        val_words_g = reuse.tile([P, I], U16, name="val_words_g", align_bytes=64, offset=T // 2)
        nc.vector.tensor_copy(val_words_g[:], val_words[:].indirect(offsets[:]))
        val_bytes_g = sb.tile([P, I], U8, name="val_bytes_g", tag="key_bytes_g", align_bytes=64)
        c0 = ps.tile([P, I], F32, name="c0")
        for cols in (lo, hi):
            nc.vector.tensor_copy(val_bytes_g[:, cols], val_bytes[:].indirect(offsets[:, cols.start // 16:cols.stop // 16]))
            product(c0[:, cols], g, val_words_g[:, cols], val_bytes_g[:, cols])

        neg_log_p = row("neg_log_p")
        nc.gpsimd.tensor_tensor(neg_log_p[:], log_u[:], neg_half[:], ALU.add)
        p = row("p")
        z = col("z")
        nc.scalar.activation(out=p[:], in_=neg_log_p[:], func=ACT.Exp, scale=-1.0, bias=shift[:], accum_out=z[:])
        nc.scalar.activation(out=r[:, lo], in_=log_u[:, lo], func=ACT.Exp, scale=-1.0)

        tilt = row("tilt", tag="val_bytes")
        nc.vector.scalar_tensor_tensor(tilt[:, hi], dl_hi[:], sharp_col[:], r[:, hi], ALU.mult, ALU.mult)
        rz = col("rz")
        nc.vector.reciprocal(rz[:], z[:])
        cp = row("cp")
        mean = col("mean")
        nc.vector.scalar_tensor_tensor(cp[:], c0[:], rz[:], p[:], ALU.mult, ALU.mult, accum_out=mean[:])
        nc.vector.scalar_tensor_tensor(tilt[:, lo], dl_lo[:], sharp_col[:], r[:, lo], ALU.mult, ALU.mult)
        weight = row("weight")
        nc.scalar.activation(out=weight[:], in_=p[:], func=ACT.Copy, scale=rz[:])
        dp = row("dp")
        nc.scalar.activation(out=dp[:], in_=c0[:], func=ACT.Identity, scale=-1.0, bias=mean[:])
        w = row("w")
        nc.vector.scalar_tensor_tensor(w[:], tilt[:], -0.25, weight[:], ALU.add, ALU.mult)

        nc.vector.tensor_tensor(window[:].indirect(offsets[:]), dp[:], w[:], ALU.mult)

        for c in range(len(OUT_EDGES) - 1):
            cols = slice(OUT_EDGES[c], OUT_EDGES[c + 1])
            total = sb.tile([P, cols.stop - cols.start], F32, name="total%d" % c)
            nc.vector.tensor_tensor(total[:], window[:, cols], old_sb[:, cols], ALU.add)
            nc.sync.dma_start(out=out[:, cols], in_=total[:])
